import numpy as np, ml_dtypes
CORES = [10,34,74,98]
N = 4
import mx_ref
BF = ml_dtypes.bfloat16
def entries(a):
    return np.ascontiguousarray(a.T).reshape(-1)
def table(e):
    return np.ascontiguousarray(np.reshape(e, (-1, 16)).T).astype(np.int32)
def gcols(t, e):
    v = np.concatenate([t.reshape(8, 16, -1, 4), np.zeros((8, 16, 1, 4), BF)], axis=2)
    return np.ascontiguousarray(np.stack([v[g][:, e[g]] for g in range(8)])).reshape(128, -1)
def cut(t, i, w=512):
    return t[:, w * i:w * i + w]
def f(rng, *shape):
    return mx_ref.flush((rng.standard_normal(shape, dtype=np.float32) * np.exp2(rng.integers(-2, 3, shape[:-1] + (1,)))).astype(BF))
def wide(rng, *shape, cols=0):
    v = rng.standard_normal(shape, dtype=np.float32) * np.exp2(rng.integers(-12, 13, shape)).astype(np.float32)
    if cols: v *= np.repeat(np.exp2(rng.integers(-cols, cols + 1, shape[:-2] + (1, shape[-1] // 4))) * (rng.random(shape[:-2] + (1, shape[-1] // 4)) > 0.0625), 4, axis=-1).astype(np.float32)
    return mx_ref.flush(v.astype(BF))
K, T, O = 512, 512, 3
SH = (7, 6, 5, 4, 3, 2, 1, 0)
A = (1531, 797, 1877, 1129, 619, 1993, 1367, 911)
B = (1013, 1741, 587, 1459, 1907, 733, 1229, 1667)
def levels(q):
    return list(range(8 // N * q, 8 // N * (q + 1)))
def owned(t):
    t = t.reshape(N, 8, 16, -1).copy()
    for q in range(N):
        for g in range(8):
            if g not in levels(q): t[q, g] = 0
    return t.reshape(N, 128, -1)
def pack(p):
    return np.stack([table(p[r]) for r in range(N)])
def places(rng):
    return {"px": pack(rng.integers(0, 1024, (N, T))), "py": pack(rng.integers(0, 1024, (N, T)))}
def setup_inputs(rng):
    return {"tb": owned(f(rng, N, 128, 4 * K)), **places(rng), "w": f(rng, N, 128, 512 * O)}
def setup_inputs_same(rng):
    d = setup_inputs(rng)
    d["px"] = pack(np.repeat(rng.integers(0, 1024, (N, 1)), T, axis=1)); d["py"] = pack(np.repeat(rng.integers(0, 1024, (N, 1)), T, axis=1))
    return d
def setup_inputs_corner(rng):
    d = setup_inputs(rng); c = rng.integers(0, 4, (N, T))
    for r in range(N): c[r, rng.permutation(T)[:4]] = np.arange(4)
    d["px"] = pack((c & 1) * 1023); d["py"] = pack((c >> 1) * 1023)
    return d
def setup_inputs_alike(rng):
    d = setup_inputs(rng)
    d["px"] = pack(np.repeat(rng.integers(0, 1024, (1, T)), N, axis=0)); d["py"] = pack(np.repeat(rng.integers(0, 1024, (1, T)), N, axis=0))
    return d
def setup_inputs_line(rng):
    d = setup_inputs(rng)
    d["px"] = pack(rng.integers(0, 1025 - T, (N, 1)) + np.arange(T)); d["py"] = pack(np.repeat(rng.integers(0, 1024, (N, 1)), T, axis=1))
    return d
def setup_inputs_spread(rng):
    d = setup_inputs(rng); d["tb"] = owned(wide(rng, N, 128, 4 * K, cols=4)); return d
def check_inputs(d):
    b = []
    for r in range(N):
        for n in ("px", "py"):
            e = entries(d[n][r])
            if e.min() < 0 or e.max() > 1023: b.append(n)
        t = d["tb"][r].reshape(8, 16, -1).astype(np.float32)
        if any((t[g] != 0).any() for g in range(8) if g not in levels(r)): b.append("tb")
    return b
def addresses(x, y):
    return np.stack([((x >> SH[g]) * A[g] + (y >> SH[g]) * B[g]) & (K - 1) for g in range(8)])
def reference(tb, px, py, w):
    y = np.zeros((N, 128, O * T), np.float32)
    for r in range(N):
        e = addresses(entries(px[r]), entries(py[r])); E = []
        for q in range(N):
            a = np.full((8, T), -1); a[levels(q)] = e[levels(q)]
            E.append(mx_ref.quantize(np.ascontiguousarray(gcols(tb[q], a))))
        for o in range(O):
            W = mx_ref.quantize(np.ascontiguousarray(cut(w[r], o)))
            Z = mx_ref.matmul(W, E[0])
            for q in range(1, N): Z = Z + mx_ref.matmul(W, E[q])
            y[r][:, T * o:T * o + T] = Z
    return {"y": y}

@@ -1,0 +1,232 @@
+import numpy as np
+from concourse.bass import DstId, RemoteDMATransfer
+from concourse.mybir import dt, AluOpType, ActivationFunctionType
+
+N = 4
+O = 3
+SH = (7, 6, 5, 4, 3, 2, 1, 0)
+MA = (1531, 797, 1877, 1129, 619, 1993, 1367, 911)
+MB = (1013, 1741, 587, 1459, 1907, 733, 1229, 1667)
+K = 512
+F8 = "float8_e4m3fn_x4"
+
+SCRATCH = {
+    "cx": ("sbuf", [128, 8], "int32"), "cy": ("sbuf", [128, 8], "int32"),
+    "lin": ("sbuf", [128, 64], "uint16"),
+    "pw": ("sbuf", [128, 64], "int32"), "lw": ("sbuf", [128, 64], "int32"), "ab": ("sbuf", [128, 64], "float32"),
+    "sc": ("sbuf", [128, 1], "float32"), "bc": ("sbuf", [128, 1], "float32"),
+    "xs": ("sbuf", [128, 64], "int32"), "xm": ("sbuf", [128, 64], "float32"),
+    "xa": ("sbuf", [128, 32], "int32"), "adr": ("sbuf", [128, 32], "int32"),
+    "tbl": ("sbuf", [128, 4 * K], "bfloat16"),
+    "part": ("sbuf", [128, 768], "float32"),
+    "yb": ("sbuf", [128, 1536], "float32"),
+    "acc": ("psum", [128, 4096], "float32"),
+}
+for _t in range(4):
+    SCRATCH["off%d" % _t] = ("sbuf", [128, 32], "uint16")
+for _s in range(4):
+    SCRATCH["wa%d" % _s] = ("sbuf", [128, 1536], "bfloat16")
+    SCRATCH["wb%d" % _s] = ("sbuf", [128, 1536], "bfloat16")
+for _k in range(4):
+    SCRATCH["eb%d" % _k] = ("sbuf", [128, 512], "bfloat16")
+    SCRATCH["eq%d" % _k] = ("sbuf", [128, 128], F8)
+    SCRATCH["es%d" % _k] = ("sbuf", [128, 128], "uint8")
+    if _k:
+        SCRATCH["rq%d" % _k] = ("sbuf", [128, 128], F8)
+        SCRATCH["rs%d" % _k] = ("sbuf", [128, 128], "uint8")
+    for _s in range(4):
+        SCRATCH["wq%d%d" % (_k, _s)] = ("sbuf", [128, 384], F8)
+        SCRATCH["ws%d%d" % (_k, _s)] = ("sbuf", [128, 384], "uint8")
+
+SEMAPHORES = (["lx", "ly", "tbs", "iot", "ct", "cv", "ad", "larr", "lsent", "esent", "rv", "pr", "pp", "pb", "pc",
+               "vb", "vf", "sf", "ys"]
+              + ["of%d" % t for t in range(4)]
+              + ["%s%d" % (n, k) for n in ("fa", "fb", "da", "db", "gv", "gs", "qe", "qw") for k in range(4)]
+              + ["arr%d" % k for k in (1, 2, 3)])
+
+ADD, MUL, AND = AluOpType.add, AluOpType.mult, AluOpType.bitwise_and
+COPY = ActivationFunctionType.Copy
+
+
+def rank_program(g, core, T, topo):
+    r = T.rank_of(core)
+    if r is None:
+        return
+    S = T.sem
+    V, A, P, Y = g.vector, g.scalar, g.tensor, g.sync
+    ks = sorted((1, 2, 3), key=lambda k: topo.same_plane(topo.chip(core), topo.chip(T.cores[r ^ k])))
+    k1, k2, k3 = ks
+
+    for s in range(4):
+        for l in range(2):
+            p = 32 * s + 16 * l
+            Y.dma_start(T.cx[p:p + 16, :], T.px[:, 8 * s:8 * s + 8]).then_inc(S.lx, 16)
+            A.dma_start(T.cy[p:p + 16, :], T.py[:, 8 * s:8 * s + 8]).then_inc(S.ly, 16)
+    for s in range(4):
+        Y.dma_start(T.tbl[32 * s:32 * s + 32, :], T.tb[32 * r:32 * r + 32, :]).then_inc(S.tbs, 16)
+
+    def load_w(name, sem, s, k):
+        q = r ^ k
+        Y.dma_start(T["%s%d" % (name, s)][32 * s:32 * s + 32, :], T.w[32 * q:32 * q + 32, :]).then_inc(S["%s%d" % (sem, s)], 16)
+
+    for s in range(4):
+        Y.wait_ge(S["fa%d" % s], 1)
+        load_w("wa", "da", s, 0)
+    for s in (1, 2, 3, 0):
+        Y.wait_ge(S["fb%d" % s], 1)
+        load_w("wb", "db", s, k1)
+    for s in range(4):
+        Y.wait_ge(S.qw0, s + 1)
+        load_w("wa", "da", s, k2)
+    for s in range(4):
+        Y.wait_ge(S["qw%d" % k1], s + 1)
+        load_w("wb", "db", s, k3)
+
+    g.iota(T.pw[:], [[0, 64]], 0, 1).then_inc(S.iot, 1)
+    dsts = [T.cores[r ^ k] for k in ks]
+    mask = topo.mask(core, dsts[0])
+    for d in dsts:
+        mask &= topo.mask(core, d)
+    ne = bin(mask).count("1")
+    g.wait_ge(S.cv, 2)
+    g.remote_dma_fused([RemoteDMATransfer(
+        dst_ids=[DstId(rid=topo.addr(d)[0], pnc=topo.addr(d)[1]) for d in dsts], dma_engine_mask=mask,
+        remote_sem=S.larr, srcs=[T.lin[:, 0:16]], dsts=[T.lin[:, 16 * k:16 * k + 16] for k in ks])], local_sem=S.lsent)
+    for k, d in zip(ks, dsts):
+        rid, pid, _ = topo.addr(d)
+        g.wait_ge(S["qe%d" % k], 1)
+        g.remote_dma(T["rq%d" % k][:].bitcast(dt.uint8), T["eq%d" % k][:].bitcast(dt.uint8), S["arr%d" % k], S.esent, pid, rid, mask)
+        g.remote_dma(T["rs%d" % k][:], T["es%d" % k][:], S["arr%d" % k], S.esent, pid, rid, mask)
+    g.wait_ge(S.lsent, ne)
+    g.wait_ge(S.esent, 6 * ne)
+
+    V.memset(T.wb0[:], 0.0).then_inc(S.fb0, 1)
+    g0, g1 = 2 * r, 2 * r + 1
+    s0, s1 = 2.0 ** -SH[g0], 2.0 ** -SH[g1]
+    V.wait_ge(S.iot, 1)
+    V.tensor_scalar(T.lw[:], T.pw[:], 16, None, AND).then_inc(S.ct, 1)
+    V.wait_ge(S.ct, 1)
+    V.tensor_scalar(T.ab[:, 0:64:2], T.lw[:, 0:64:2], (MA[g1] - MA[g0]) / 4.0, 4.0 * MA[g0], MUL, ADD).then_inc(S.ct, 1)
+    V.tensor_scalar(T.ab[:, 1:64:2], T.lw[:, 1:64:2], (MB[g1] - MB[g0]) / 4.0, 4.0 * MB[g0], MUL, ADD).then_inc(S.ct, 1)
+    V.tensor_scalar(T.sc[:], T.lw[:, 0:1], (s1 - s0) / 16.0, s0, MUL, ADD).then_inc(S.ct, 1)
+    V.tensor_scalar(T.bc[:], T.lw[:, 0:1], (s1 - s0) / 32.0, (s0 - 1.0) / 2.0, MUL, ADD).then_inc(S.ct, 1)
+    V.memset(T.wa0[:], 0.0).then_inc(S.fa0, 1)
+    V.wait_ge(S.lx, 128)
+    V.tensor_copy(T.lin[:, 0:16:2], T.cx[:]).then_inc(S.cv, 1)
+    V.wait_ge(S.ly, 128)
+    V.tensor_copy(T.lin[:, 1:16:2], T.cy[:]).then_inc(S.cv, 1)
+    for s in (1, 2, 3):
+        V.memset(T["wa%d" % s][:], 0.0).then_inc(S["fa%d" % s], 1)
+
+    def quant_w(name, sem, k, val):
+        for s in range(4):
+            V.wait_ge(S["%s%d" % (sem, s)], val)
+            V.quantize_mx(T["wq%d%d" % (k, s)][:], T["ws%d%d" % (k, s)][:], T["%s%d" % (name, s)][:]).then_inc(S["qw%d" % k], 1)
+
+    quant_w("wa", "da", 0, 16)
+    V.wait_ge(S.cv, 2)
+    V.wait_ge(S.ct, 5)
+    V.wait_ge(S.larr, 3 * ne)
+    V.tensor_scalar(T.xs[:], T.lin[:], T.sc[:], T.bc[:], MUL, ADD).then_inc(S.ad, 1)
+    V.wait_ge(S.ad, 1)
+    V.tensor_tensor(T.xm[:], T.xs[:], T.ab[:], MUL).then_inc(S.ad, 1)
+    V.wait_ge(S.ad, 2)
+    V.tensor_tensor(T.xa[:], T.xm[:, 0:64:2], T.xm[:, 1:64:2], ADD).then_inc(S.ad, 1)
+    V.wait_ge(S.ad, 3)
+    V.tensor_scalar(T.adr[:], T.xa[:], 4 * (K - 1), None, AND).then_inc(S.ad, 1)
+    V.wait_ge(S.ad, 4)
+    for t in (2, 0, 3, 1):
+        V.tensor_scalar(T["off%d" % t][:], T.adr[:], float(t), None, ADD).then_inc(S["of%d" % t], 1)
+    V.wait_ge(S.tbs, 64)
+    V.wait_ge(S.of0, 1)
+    V.wait_ge(S.of1, 1)
+    for k in ks + [0]:
+        for t in (0, 1):
+            V.tensor_copy(T["eb%d" % k][:, t:512:4], T.tbl[:].indirect(T["off%d" % t][:, 8 * k:8 * k + 8])).then_inc(S["gv%d" % k], 1)
+        V.wait_ge(S["gv%d" % k], 2)
+        V.wait_ge(S["gs%d" % k], 2)
+        V.quantize_mx(T["eq%d" % k][:], T["es%d" % k][:], T["eb%d" % k][:]).then_inc(S["qe%d" % k], 1)
+    quant_w("wb", "db", k1, 16)
+    quant_w("wa", "da", k2, 32)
+    quant_w("wb", "db", k3, 32)
+
+    A.wait_ge(S.fb0, 1)
+    for s in (1, 2, 3):
+        A.activation(T["wb%d" % s][:], T.wb0[:], COPY).then_inc(S["fb%d" % s], 1)
+    A.wait_ge(S.tbs, 64)
+    A.wait_ge(S.of2, 1)
+    for n, k in enumerate(ks + [0]):
+        for t in (2, 3):
+            if n == 0 and t == 3:
+                A.wait_ge(S.of3, 1)
+            A.activation(T["eb%d" % k][:, t:512:4], T.tbl[:].indirect(T["off%d" % t][:, 8 * k:8 * k + 8]), COPY).then_inc(S["gs%d" % k], 1)
+
+    keep = [(o, s) for o in range(O) for s in (0, 1)]
+    pas = [(o, s) for o in range(O) for s in (2, 3)]
+
+    def bank(b):
+        return T.acc[:, 512 * b:512 * b + 128]
+
+    def mm(b, k, o, s, start, stop):
+        e, z = (("rq%d", "rs%d") if k else ("eq%d", "es%d"))
+        c = slice(128 * o, 128 * o + 128)
+        return P.matmul_mx(bank(b), T["wq%d%d" % (k, s)][:, c], T["ws%d%d" % (k, s)][:, c], T[e % k][:], T[z % k][:], start, stop)
+
+    def ready(k):
+        P.wait_ge(S["qw%d" % k], 4)
+        if k:
+            P.wait_ge(S["arr%d" % k], 2 * ne)
+        else:
+            P.wait_ge(S.qe0, 1)
+
+    ready(0)
+    for j in range(6):
+        o, s = keep[j]
+        mm(j, 0, o, s, True, False)
+        if j >= 2:
+            P.wait_ge(S.rv, j - 1)
+        o, s = pas[j]
+        mm(6 + j % 2, 0, o, s, True, True).then_inc(S.pr, 1)
+    ready(k1)
+    for j in range(6):
+        mm(j, k1, keep[j][0], keep[j][1], False, False)
+    ready(k2)
+    for j in range(6):
+        mm(j, k2, keep[j][0], keep[j][1], False, False)
+        if j < 2:
+            P.wait_ge(S.rv, 5 + j)
+        else:
+            P.wait_ge(S.vb, j - 1)
+        mm(6 + j % 2, k1, pas[j][0], pas[j][1], True, False)
+        mm(6 + j % 2, k2, pas[j][0], pas[j][1], False, True).then_inc(S.pb, 1)
+    ready(k3)
+    for j in range(6):
+        mm(j, k3, keep[j][0], keep[j][1], False, True).then_inc(S.pp, 1)
+        if j < 2:
+            P.wait_ge(S.vb, 5 + j)
+        else:
+            P.wait_ge(S.vf, j - 1)
+        mm(6 + j % 2, k3, pas[j][0], pas[j][1], True, True).then_inc(S.pc, 1)
+
+    def ycol(o, s):
+        return T.yb[:, 512 * o + 128 * s:512 * o + 128 * s + 128]
+
+    for j in range(6):
+        A.wait_ge(S.pr, j + 1)
+        A.activation(T.part[:, 128 * j:128 * j + 128], bank(6 + j % 2), COPY).then_inc(S.rv, 1)
+    for j in range(6):
+        pj = T.part[:, 128 * j:128 * j + 128]
+        V.wait_ge(S.pb, j + 1)
+        V.wait_ge(S.rv, j + 1)
+        V.tensor_tensor(pj, bank(6 + j % 2), pj, ADD).then_inc(S.vb, 1)
+    for j in range(6):
+        A.wait_ge(S.pp, j + 1)
+        A.activation(ycol(*keep[j]), bank(j), COPY).then_inc(S.sf, 1)
+        V.wait_ge(S.pc, j + 1)
+        V.wait_ge(S.vb, j + 1)
+        V.tensor_tensor(ycol(*pas[j]), bank(6 + j % 2), T.part[:, 128 * j:128 * j + 128], ADD).then_inc(S.vf, 1)
+    for o in range(O):
+        Y.wait_ge(S.sf, 2 * o + 2)
+        Y.wait_ge(S.vf, 2 * o + 2)
+        Y.dma_start(T.y[:, 512 * o:512 * o + 512], T.yb[:, 512 * o:512 * o + 512]).then_inc(S.ys, 16)
+    Y.wait_ge(S.ys, 16 * O)

@@ -1,4 +1,3 @@
-import numpy as np
 from concourse.bass import DstId, RemoteDMATransfer
 from concourse.mybir import dt, AluOpType, ActivationFunctionType
 
@@ -8,41 +7,41 @@ SH = (7, 6, 5, 4, 3, 2, 1, 0)
 MA = (1531, 797, 1877, 1129, 619, 1993, 1367, 911)
 MB = (1013, 1741, 587, 1459, 1907, 733, 1229, 1667)
 K = 512
+M0 = (0, 11, 21)
+C = 11
+NC = 16 * C
 F8 = "float8_e4m3fn_x4"
 
 SCRATCH = {
-    "cx": ("sbuf", [128, 8], "int32"), "cy": ("sbuf", [128, 8], "int32"),
-    "lin": ("sbuf", [128, 64], "uint16"),
-    "pw": ("sbuf", [128, 64], "int32"), "lw": ("sbuf", [128, 64], "int32"), "ab": ("sbuf", [128, 64], "float32"),
-    "sc": ("sbuf", [128, 1], "float32"), "bc": ("sbuf", [128, 1], "float32"),
-    "xs": ("sbuf", [128, 64], "int32"), "xm": ("sbuf", [128, 64], "float32"),
-    "xa": ("sbuf", [128, 32], "int32"), "adr": ("sbuf", [128, 32], "int32"),
-    "tbl": ("sbuf", [128, 4 * K], "bfloat16"),
-    "part": ("sbuf", [128, 768], "float32"),
-    "yb": ("sbuf", [128, 1536], "float32"),
+    "cxy": ("sbuf", [128, 64], "int32"),
+    "pw": ("sbuf", [128, 16], "int32"), "lw": ("sbuf", [128, 16], "int32"), "ab": ("sbuf", [128, 8 * C], "float32"),
+    "sc": ("sbuf", [128, 4], "float32"), "bc": ("sbuf", [128, 4], "float32"),
+    "xs": ("sbuf", [128, 8 * C], "int32"), "xm": ("sbuf", [128, 8 * C], "float32"),
+    "xa": ("sbuf", [128, 4 * C], "int32"), "adr": ("sbuf", [128, 4 * C], "int32"),
+    "lout": ("sbuf", [128, 48], "uint16"), "lin": ("sbuf", [128, 48], "uint16"),
+    "tbl": ("sbuf", [128, 4 * K], "bfloat16"), "zb": ("sbuf", [128, 512], "bfloat16"),
+    "yb": ("sbuf", [128, 1536], "float32"), "part": ("sbuf", [128, 2 * NC], "float32"),
     "acc": ("psum", [128, 4096], "float32"),
 }
-for _t in range(4):
-    SCRATCH["off%d" % _t] = ("sbuf", [128, 32], "uint16")
-for _s in range(4):
-    SCRATCH["wa%d" % _s] = ("sbuf", [128, 1536], "bfloat16")
-    SCRATCH["wb%d" % _s] = ("sbuf", [128, 1536], "bfloat16")
+for _t in (1, 2, 3):
+    SCRATCH["off%d" % _t] = ("sbuf", [128, 48], "uint16")
+for _i in range(6):
+    SCRATCH["wt%d" % _i] = ("sbuf", [128, 1536], "bfloat16")
+    SCRATCH["wq%d" % _i] = ("sbuf", [128, 384], F8)
+    SCRATCH["ws%d" % _i] = ("sbuf", [128, 384], "uint8")
 for _k in range(4):
-    SCRATCH["eb%d" % _k] = ("sbuf", [128, 512], "bfloat16")
-    SCRATCH["eq%d" % _k] = ("sbuf", [128, 128], F8)
-    SCRATCH["es%d" % _k] = ("sbuf", [128, 128], "uint8")
+    SCRATCH["eb%d" % _k] = ("sbuf", [128, 4 * NC], "bfloat16")
+    SCRATCH["eq%d" % _k] = ("sbuf", [128, NC], F8)
+    SCRATCH["es%d" % _k] = ("sbuf", [128, NC], "uint8")
     if _k:
-        SCRATCH["rq%d" % _k] = ("sbuf", [128, 128], F8)
-        SCRATCH["rs%d" % _k] = ("sbuf", [128, 128], "uint8")
-    for _s in range(4):
-        SCRATCH["wq%d%d" % (_k, _s)] = ("sbuf", [128, 384], F8)
-        SCRATCH["ws%d%d" % (_k, _s)] = ("sbuf", [128, 384], "uint8")
+        SCRATCH["rq%d" % _k] = ("sbuf", [128, NC], F8)
+        SCRATCH["rs%d" % _k] = ("sbuf", [128, NC], "uint8")
 
-SEMAPHORES = (["lx", "ly", "tbs", "iot", "ct", "cv", "ad", "larr", "lsent", "esent", "rv", "pr", "pp", "pb", "pc",
-               "vb", "vf", "sf", "ys"]
-              + ["of%d" % t for t in range(4)]
-              + ["%s%d" % (n, k) for n in ("fa", "fb", "da", "db", "gv", "gs", "qe", "qw") for k in range(4)]
-              + ["arr%d" % k for k in (1, 2, 3)])
+SEMAPHORES = (["lx", "ly", "fz", "tbs", "iot", "ct", "cd", "ad", "lo", "lown", "larr", "lsent", "esent",
+               "pr", "rv", "pb", "vb", "sf", "vf", "ys"]
+              + ["%s%d" % (n, k) for n in ("gv", "gs", "qe", "oo", "oi", "arr") for k in range(4)]
+              + ["%s%d" % (n, i) for n in ("fw", "dw", "qw") for i in range(6)]
+              + ["pp%d" % b for b in range(9)])
 
 ADD, MUL, AND = AluOpType.add, AluOpType.mult, AluOpType.bitwise_and
 COPY = ActivationFunctionType.Copy
@@ -56,177 +55,240 @@ def rank_program(g, core, T, topo):
     V, A, P, Y = g.vector, g.scalar, g.tensor, g.sync
     ks = sorted((1, 2, 3), key=lambda k: topo.same_plane(topo.chip(core), topo.chip(T.cores[r ^ k])))
     k1, k2, k3 = ks
+    q1, q2, q3 = [r ^ k for k in ks]
+    tiles = [{r, q1}, {r, q2}, {r, q3}, {q1, q2}, {q1, q3}, {q2, q3}]
+    dsts = [T.cores[q] for q in (q1, q2, q3)]
+    engs = [e for e in topo.engines(core, dsts[0]) if all(e in topo.engines(core, d) for d in dsts)]
+    ne = len(engs)
+    mask = sum(1 << e for e in engs)
+    parts = [engs[0::2], engs[1::4], engs[3::4]]
 
     for s in range(4):
         for l in range(2):
             p = 32 * s + 16 * l
-            Y.dma_start(T.cx[p:p + 16, :], T.px[:, 8 * s:8 * s + 8]).then_inc(S.lx, 16)
-            A.dma_start(T.cy[p:p + 16, :], T.py[:, 8 * s:8 * s + 8]).then_inc(S.ly, 16)
+            if s < 3:
+                m = M0[s]
+                Y.dma_start(T.cxy[p:p + 16, 0:C], T.px[:, m:m + C]).then_inc(S.lx, 16)
+                A.dma_start(T.cxy[p:p + 16, C:2 * C], T.py[:, m:m + C]).then_inc(S.ly, 16)
+            else:
+                Y.dma_start(T.cxy[p:p + 16, 0:32], T.px[:]).then_inc(S.lx, 16)
+                A.dma_start(T.cxy[p:p + 16, 32:64], T.py[:]).then_inc(S.ly, 16)
     for s in range(4):
-        Y.dma_start(T.tbl[32 * s:32 * s + 32, :], T.tb[32 * r:32 * r + 32, :]).then_inc(S.tbs, 16)
+        q = r if s != r else (r + 1) % N
+        Y.dma_start(T.tbl[32 * s:32 * s + 32, :], T.tb[32 * q:32 * q + 32, :]).then_inc(S.tbs, 16)
 
-    def load_w(name, sem, s, k):
-        q = r ^ k
-        Y.dma_start(T["%s%d" % (name, s)][32 * s:32 * s + 32, :], T.w[32 * q:32 * q + 32, :]).then_inc(S["%s%d" % (sem, s)], 16)
+    def wload(i, n):
+        Y.wait_ge(S["fw%d" % i], n)
+        a, b = sorted(tiles[i])
+        for q, s in ((a, b), (b, a)):
+            Y.dma_start(T["wt%d" % i][32 * s:32 * s + 32, :], T.w[32 * q:32 * q + 32, :]).then_inc(S["dw%d" % i], 16)
 
-    for s in range(4):
-        Y.wait_ge(S["fa%d" % s], 1)
-        load_w("wa", "da", s, 0)
-    for s in (1, 2, 3, 0):
-        Y.wait_ge(S["fb%d" % s], 1)
-        load_w("wb", "db", s, k1)
-    for s in range(4):
-        Y.wait_ge(S.qw0, s + 1)
-        load_w("wa", "da", s, k2)
-    for s in range(4):
-        Y.wait_ge(S["qw%d" % k1], s + 1)
-        load_w("wb", "db", s, k3)
+    wload(0, 1)
+    wload(2, 3)
+    wload(1, 2)
+    Y.wait_ge(S.lsent, ne)
+    for i, n in ((3, 3), (4, 3), (5, 1)):
+        wload(i, n)
 
-    g.iota(T.pw[:], [[0, 64]], 0, 1).then_inc(S.iot, 1)
-    dsts = [T.cores[r ^ k] for k in ks]
-    mask = topo.mask(core, dsts[0])
-    for d in dsts:
-        mask &= topo.mask(core, d)
-    ne = bin(mask).count("1")
-    g.wait_ge(S.cv, 2)
-    g.remote_dma_fused([RemoteDMATransfer(
-        dst_ids=[DstId(rid=topo.addr(d)[0], pnc=topo.addr(d)[1]) for d in dsts], dma_engine_mask=mask,
-        remote_sem=S.larr, srcs=[T.lin[:, 0:16]], dsts=[T.lin[:, 16 * k:16 * k + 16] for k in ks])], local_sem=S.lsent)
+    g.iota(T.pw[:], [[0, 16]], 0, 1).then_inc(S.iot, 1)
+    trs = []
+    for k, q, d, es in zip(ks, (q1, q2, q3), dsts, parts):
+        rid, pid, _ = topo.addr(d)
+        trs.append(RemoteDMATransfer(
+            dst_ids=[DstId(rid=rid, pnc=pid)], dma_engine_mask=sum(1 << e for e in es), remote_sem=S.larr,
+            srcs=[T.lout[:, 12 * q:12 * q + 12]], dsts=[T.lin[:, 12 * k:12 * k + 12]]))
+    g.wait_ge(S.lo, 3)
+    g.remote_dma_fused(trs, local_sem=S.lsent)
     for k, d in zip(ks, dsts):
         rid, pid, _ = topo.addr(d)
         g.wait_ge(S["qe%d" % k], 1)
         g.remote_dma(T["rq%d" % k][:].bitcast(dt.uint8), T["eq%d" % k][:].bitcast(dt.uint8), S["arr%d" % k], S.esent, pid, rid, mask)
         g.remote_dma(T["rs%d" % k][:], T["es%d" % k][:], S["arr%d" % k], S.esent, pid, rid, mask)
-    g.wait_ge(S.lsent, ne)
     g.wait_ge(S.esent, 6 * ne)
 
-    V.memset(T.wb0[:], 0.0).then_inc(S.fb0, 1)
-    g0, g1 = 2 * r, 2 * r + 1
-    s0, s1 = 2.0 ** -SH[g0], 2.0 ** -SH[g1]
+    V.memset(T.zb[:], 0.0).then_inc(S.fz, 1)
+    V.memset(T.wt0[:], 0.0).then_inc(S.fw0, 1)
+    V.memset(T.lout[:], 0).then_inc(S.cd, 1)
+    V.memset(T.xs[96:128, :], 0).then_inc(S.cd, 1)
     V.wait_ge(S.iot, 1)
     V.tensor_scalar(T.lw[:], T.pw[:], 16, None, AND).then_inc(S.ct, 1)
     V.wait_ge(S.ct, 1)
-    V.tensor_scalar(T.ab[:, 0:64:2], T.lw[:, 0:64:2], (MA[g1] - MA[g0]) / 4.0, 4.0 * MA[g0], MUL, ADD).then_inc(S.ct, 1)
-    V.tensor_scalar(T.ab[:, 1:64:2], T.lw[:, 1:64:2], (MB[g1] - MB[g0]) / 4.0, 4.0 * MB[g0], MUL, ADD).then_inc(S.ct, 1)
-    V.tensor_scalar(T.sc[:], T.lw[:, 0:1], (s1 - s0) / 16.0, s0, MUL, ADD).then_inc(S.ct, 1)
-    V.tensor_scalar(T.bc[:], T.lw[:, 0:1], (s1 - s0) / 32.0, (s0 - 1.0) / 2.0, MUL, ADD).then_inc(S.ct, 1)
-    V.memset(T.wa0[:], 0.0).then_inc(S.fa0, 1)
+    for q in range(N):
+        a, b = 2 * q, 2 * q + 1
+        V.tensor_scalar(T.sc[:, q:q + 1], T.lw[:, 0:1], 2.0 ** -SH[a] / 16.0, 2.0 ** -SH[a], MUL, ADD).then_inc(S.cd, 1)
+        for c, M in ((0, MA), (4 * C, MB)):
+            V.tensor_scalar(T.ab[:, c + q:c + 4 * C:4], T.lw[:, 0:C], (M[b] - M[a]) / 4.0, 4.0 * M[a], MUL, ADD).then_inc(S.cd, 1)
+    V.wait_ge(S.cd, 14)
+    V.tensor_scalar(T.bc[:], T.sc[:], 0.5, -0.5, MUL, ADD).then_inc(S.cd, 1)
+    V.memset(T.wt1[:, 0:512], 0.0).then_inc(S.fw1, 1)
+    V.wait_ge(S.cd, 15)
     V.wait_ge(S.lx, 128)
-    V.tensor_copy(T.lin[:, 0:16:2], T.cx[:]).then_inc(S.cv, 1)
     V.wait_ge(S.ly, 128)
-    V.tensor_copy(T.lin[:, 1:16:2], T.cy[:]).then_inc(S.cv, 1)
-    for s in (1, 2, 3):
-        V.memset(T["wa%d" % s][:], 0.0).then_inc(S["fa%d" % s], 1)
-
-    def quant_w(name, sem, k, val):
-        for s in range(4):
-            V.wait_ge(S["%s%d" % (sem, s)], val)
-            V.quantize_mx(T["wq%d%d" % (k, s)][:], T["ws%d%d" % (k, s)][:], T["%s%d" % (name, s)][:]).then_inc(S["qw%d" % k], 1)
-
-    quant_w("wa", "da", 0, 16)
-    V.wait_ge(S.cv, 2)
-    V.wait_ge(S.ct, 5)
-    V.wait_ge(S.larr, 3 * ne)
-    V.tensor_scalar(T.xs[:], T.lin[:], T.sc[:], T.bc[:], MUL, ADD).then_inc(S.ad, 1)
-    V.wait_ge(S.ad, 1)
+    for q in range(N):
+        V.tensor_scalar(T.xs[0:96, q:8 * C:4], T.cxy[0:96, 0:2 * C], T.sc[0:96, q:q + 1], T.bc[0:96, q:q + 1], MUL, ADD).then_inc(S.ad, 1)
+        if q < 3:
+            m = M0[q]
+            for c, x in ((0, m), (4 * C, 32 + m)):
+                V.tensor_scalar(T.xs[96:128, c + q:c + 4 * C:4], T.cxy[96:128, x:x + C], T.sc[96:128, q:q + 1], T.bc[96:128, q:q + 1], MUL, ADD).then_inc(S.ad, 1)
+    V.wait_ge(S.ad, 10)
     V.tensor_tensor(T.xm[:], T.xs[:], T.ab[:], MUL).then_inc(S.ad, 1)
-    V.wait_ge(S.ad, 2)
-    V.tensor_tensor(T.xa[:], T.xm[:, 0:64:2], T.xm[:, 1:64:2], ADD).then_inc(S.ad, 1)
-    V.wait_ge(S.ad, 3)
+    V.wait_ge(S.ad, 11)
+    V.tensor_tensor(T.xa[:], T.xm[:, 0:4 * C], T.xm[:, 4 * C:8 * C], ADD).then_inc(S.ad, 1)
+    V.wait_ge(S.ad, 12)
     V.tensor_scalar(T.adr[:], T.xa[:], 4 * (K - 1), None, AND).then_inc(S.ad, 1)
-    V.wait_ge(S.ad, 4)
-    for t in (2, 0, 3, 1):
-        V.tensor_scalar(T["off%d" % t][:], T.adr[:], float(t), None, ADD).then_inc(S["of%d" % t], 1)
-    V.wait_ge(S.tbs, 64)
-    V.wait_ge(S.of0, 1)
-    V.wait_ge(S.of1, 1)
-    for k in ks + [0]:
-        for t in (0, 1):
-            V.tensor_copy(T["eb%d" % k][:, t:512:4], T.tbl[:].indirect(T["off%d" % t][:, 8 * k:8 * k + 8])).then_inc(S["gv%d" % k], 1)
-        V.wait_ge(S["gv%d" % k], 2)
-        V.wait_ge(S["gs%d" % k], 2)
-        V.quantize_mx(T["eq%d" % k][:], T["es%d" % k][:], T["eb%d" % k][:]).then_inc(S["qe%d" % k], 1)
-    quant_w("wb", "db", k1, 16)
-    quant_w("wa", "da", k2, 32)
-    quant_w("wb", "db", k3, 32)
+    V.wait_ge(S.ad, 13)
+    for q in (q1, q2, q3, r):
+        V.tensor_copy(T.lout[:, 12 * q:12 * q + C], T.adr[:, q:4 * C:4]).then_inc(S.lown if q == r else S.lo, 1)
+    V.memset(T.wt1[:, 512:1536], 0.0).then_inc(S.fw1, 1)
 
-    A.wait_ge(S.fb0, 1)
-    for s in (1, 2, 3):
-        A.activation(T["wb%d" % s][:], T.wb0[:], COPY).then_inc(S["fb%d" % s], 1)
-    A.wait_ge(S.tbs, 64)
-    A.wait_ge(S.of2, 1)
-    for n, k in enumerate(ks + [0]):
-        for t in (2, 3):
-            if n == 0 and t == 3:
-                A.wait_ge(S.of3, 1)
-            A.activation(T["eb%d" % k][:, t:512:4], T.tbl[:].indirect(T["off%d" % t][:, 8 * k:8 * k + 8]), COPY).then_inc(S["gs%d" % k], 1)
+    def offs(t, k):
+        c = 12 * k
+        if t:
+            return T["off%d" % t][:, c:c + C]
+        return T.lin[:, c:c + C] if k else T.lout[:, 12 * r:12 * r + C]
 
-    keep = [(o, s) for o in range(O) for s in (0, 1)]
-    pas = [(o, s) for o in range(O) for s in (2, 3)]
+    V.wait_ge(S.lown, 1)
+    for t in (3, 1, 2):
+        V.tensor_scalar(T["off%d" % t][:, 0:12], T.lout[:, 12 * r:12 * r + 12], float(t), None, ADD).then_inc(S["oo%d" % t], 1)
 
-    def bank(b):
-        return T.acc[:, 512 * b:512 * b + 128]
+    def vg(k):
+        for t in (1, 2):
+            V.tensor_copy(T["eb%d" % k][:, t:4 * NC:4], T.tbl[:].indirect(offs(t, k))).then_inc(S["gv%d" % k], 1)
 
-    def mm(b, k, o, s, start, stop):
-        e, z = (("rq%d", "rs%d") if k else ("eq%d", "es%d"))
-        c = slice(128 * o, 128 * o + 128)
-        return P.matmul_mx(bank(b), T["wq%d%d" % (k, s)][:, c], T["ws%d%d" % (k, s)][:, c], T[e % k][:], T[z % k][:], start, stop)
-
-    def ready(k):
-        P.wait_ge(S["qw%d" % k], 4)
+    def vq(k):
         if k:
-            P.wait_ge(S["arr%d" % k], 2 * ne)
-        else:
-            P.wait_ge(S.qe0, 1)
+            V.wait_ge(S["gv%d" % k], 2)
+        V.wait_ge(S["gs%d" % k], 2 if k else 4)
+        V.quantize_mx(T["eq%d" % k][:], T["es%d" % k][:], T["eb%d" % k][:]).then_inc(S["qe%d" % k], 1)
 
-    ready(0)
-    for j in range(6):
-        o, s = keep[j]
-        mm(j, 0, o, s, True, False)
-        if j >= 2:
-            P.wait_ge(S.rv, j - 1)
-        o, s = pas[j]
-        mm(6 + j % 2, 0, o, s, True, True).then_inc(S.pr, 1)
-    ready(k1)
-    for j in range(6):
-        mm(j, k1, keep[j][0], keep[j][1], False, False)
-    ready(k2)
-    for j in range(6):
-        mm(j, k2, keep[j][0], keep[j][1], False, False)
-        if j < 2:
-            P.wait_ge(S.rv, 5 + j)
-        else:
-            P.wait_ge(S.vb, j - 1)
-        mm(6 + j % 2, k1, pas[j][0], pas[j][1], True, False)
-        mm(6 + j % 2, k2, pas[j][0], pas[j][1], False, True).then_inc(S.pb, 1)
-    ready(k3)
-    for j in range(6):
-        mm(j, k3, keep[j][0], keep[j][1], False, True).then_inc(S.pp, 1)
-        if j < 2:
-            P.wait_ge(S.vb, 5 + j)
-        else:
-            P.wait_ge(S.vf, j - 1)
-        mm(6 + j % 2, k3, pas[j][0], pas[j][1], True, True).then_inc(S.pc, 1)
+    def vw(i):
+        V.wait_ge(S["dw%d" % i], 32)
+        V.quantize_mx(T["wq%d" % i][:], T["ws%d" % i][:], T["wt%d" % i][:]).then_inc(S["qw%d" % i], 1)
 
-    def ycol(o, s):
-        return T.yb[:, 512 * o + 128 * s:512 * o + 128 * s + 128]
+    vw(0)
+    vw(2)
+    V.memset(T.wt5[:], 0.0).then_inc(S.fw5, 1)
+    vq(0)
+    vw(1)
+    V.wait_ge(S.tbs, 64)
+    V.wait_ge(S.larr, ne)
+    for t in (3, 1, 2):
+        V.tensor_scalar(T["off%d" % t][:, 12:48], T.lin[:, 12:48], float(t), None, ADD).then_inc(S["oi%d" % t], 1)
+    V.wait_ge(S.oi1, 1)
+    V.wait_ge(S.oi2, 1)
+    for k in ks:
+        vg(k)
+        vq(k)
+    for i in (3, 4, 5):
+        vw(i)
 
-    for j in range(6):
-        A.wait_ge(S.pr, j + 1)
-        A.activation(T.part[:, 128 * j:128 * j + 128], bank(6 + j % 2), COPY).then_inc(S.rv, 1)
-    for j in range(6):
-        pj = T.part[:, 128 * j:128 * j + 128]
-        V.wait_ge(S.pb, j + 1)
-        V.wait_ge(S.rv, j + 1)
-        V.tensor_tensor(pj, bank(6 + j % 2), pj, ADD).then_inc(S.vb, 1)
-    for j in range(6):
-        A.wait_ge(S.pp, j + 1)
-        A.activation(ycol(*keep[j]), bank(j), COPY).then_inc(S.sf, 1)
-        V.wait_ge(S.pc, j + 1)
-        V.wait_ge(S.vb, j + 1)
-        V.tensor_tensor(ycol(*pas[j]), bank(6 + j % 2), T.part[:, 128 * j:128 * j + 128], ADD).then_inc(S.vf, 1)
+    A.wait_ge(S.fz, 1)
+    for i in (2, 3, 4):
+        for c in range(0, 1536, 512):
+            A.activation(T["wt%d" % i][:, c:c + 512], T.zb[:], COPY).then_inc(S["fw%d" % i], 1)
+    A.wait_ge(S.tbs, 64)
+
+    def ag(k, t):
+        A.activation(T["eb%d" % k][:, t:4 * NC:4], T.tbl[:].indirect(offs(t, k)), COPY).then_inc(S["gs%d" % k], 1)
+
+    A.wait_ge(S.lown, 1)
+    ag(0, 0)
+    for t in (3, 1, 2):
+        A.wait_ge(S["oo%d" % t], 1)
+        ag(0, t)
+    A.wait_ge(S.larr, ne)
+    for n, k in enumerate(ks):
+        ag(k, 0)
+        if n == 0:
+            A.wait_ge(S.oi3, 1)
+        ag(k, 3)
+
+    seq = [(0, 2), (0, 0), (0, 1), (1, 0), (1, 2), (1, 1), (2, 0), (2, 1), (2, 2)]
+    pas = [(0, 2), (1, 2)]
+    keep = [x for x in seq if x not in pas]
+
+    def base(x):
+        return 512 * (7 if x in pas else keep.index(x))
+
+    seen = []
+
+    def mm(k, x, first, last):
+        e, z = ("rq%d", "rs%d") if k else ("eq%d", "es%d")
+        o, th = x
+        q = r ^ k
+        s = 3 if (th == q and q < 3) else th
+        i = tiles.index({q, s})
+        if i not in seen:
+            seen.append(i)
+            P.wait_ge(S["qw%d" % i], 1)
+        c = slice(128 * o, 128 * o + 128)
+        b = base(x)
+        return P.matmul_mx(T.acc[:, b:b + NC], T["wq%d" % i][:, c], T["ws%d" % i][:, c], T[e % k][:], T[z % k][:], first, last)
+
+    P.wait_ge(S.qe0, 1)
+    for x in seq:
+        if x in pas:
+            if x == pas[1]:
+                P.wait_ge(S.rv, 1)
+            mm(0, x, True, True).then_inc(S.pr, 1)
+        else:
+            mm(0, x, True, False)
+    P.wait_ge(S["arr%d" % k1], 2 * ne)
+    for x in keep:
+        mm(k1, x, False, False)
+    P.wait_ge(S["arr%d" % k2], 2 * ne)
+    for x in seq:
+        if x in pas:
+            if x == pas[0]:
+                P.wait_ge(S.rv, 2)
+            else:
+                P.wait_ge(S.vb, 1)
+            mm(k1, x, True, False)
+            mm(k2, x, False, True).then_inc(S.pb, 1)
+        else:
+            mm(k2, x, False, False)
+    P.wait_ge(S["arr%d" % k3], 2 * ne)
+    for n, x in enumerate(seq):
+        if x in pas:
+            if x == pas[0]:
+                P.wait_ge(S.vb, 2)
+            else:
+                P.wait_ge(S.vf, 1)
+        mm(k3, x, x in pas, True).then_inc(S["pp%d" % n], 1)
+
+    for i in range(2):
+        A.wait_ge(S.pr, i + 1)
+        A.activation(T.part[:, NC * i:NC * i + NC], T.acc[:, 3584:3584 + NC], COPY).then_inc(S.rv, 1)
+    for i in range(2):
+        pi = T.part[:, NC * i:NC * i + NC]
+        V.wait_ge(S.pb, i + 1)
+        V.wait_ge(S.rv, i + 1)
+        V.tensor_tensor(pi, T.acc[:, 3584:3584 + NC], pi, ADD).then_inc(S.vb, 1)
+    cnt = {"s": 0, "v": 0}
+    done = {}
+    for n, x in enumerate(seq):
+        o, th = x
+        lo = 0 if th < 2 else 16 * (M0[1] + C - M0[2])
+        y = T.yb[:, 512 * o + 16 * M0[th] + lo:512 * o + 16 * M0[th] + NC]
+        b = base(x)
+        a = T.acc[:, b + lo:b + NC]
+        if x in pas:
+            i = pas.index(x)
+            V.wait_ge(S["pp%d" % n], 1)
+            V.wait_ge(S.vb, i + 1)
+            V.tensor_tensor(y, a, T.part[:, NC * i + lo:NC * i + NC], ADD).then_inc(S.vf, 1)
+            cnt["v"] += 1
+        elif n % 2:
+            A.wait_ge(S["pp%d" % n], 1)
+            A.activation(y, a, COPY).then_inc(S.sf, 1)
+            cnt["s"] += 1
+        else:
+            V.wait_ge(S["pp%d" % n], 1)
+            V.tensor_copy(y, a).then_inc(S.vf, 1)
+            cnt["v"] += 1
+        done[o] = (cnt["s"], cnt["v"])
     for o in range(O):
-        Y.wait_ge(S.sf, 2 * o + 2)
-        Y.wait_ge(S.vf, 2 * o + 2)
+        Y.wait_ge(S.sf, done[o][0])
+        Y.wait_ge(S.vf, done[o][1])
         Y.dma_start(T.y[:, 512 * o:512 * o + 512], T.yb[:, 512 * o:512 * o + 512]).then_inc(S.ys, 16)
     Y.wait_ge(S.ys, 16 * O)

from concourse.bass import DstId, RemoteDMATransfer
from concourse.mybir import dt, AluOpType, ActivationFunctionType

N = 4
O = 3
SH = (7, 6, 5, 4, 3, 2, 1, 0)
MA = (1531, 797, 1877, 1129, 619, 1993, 1367, 911)
MB = (1013, 1741, 587, 1459, 1907, 733, 1229, 1667)
K = 512
M0 = (0, 11, 21)
C = 11
NC = 16 * C
F8 = "float8_e4m3fn_x4"

SCRATCH = {
    "cxy": ("sbuf", [128, 64], "int32"),
    "pw": ("sbuf", [128, 16], "int32"), "lw": ("sbuf", [128, 16], "int32"), "ab": ("sbuf", [128, 8 * C], "float32"),
    "sc": ("sbuf", [128, 4], "float32"), "bc": ("sbuf", [128, 4], "float32"),
    "xs": ("sbuf", [128, 8 * C], "int32"), "xm": ("sbuf", [128, 8 * C], "float32"),
    "xa": ("sbuf", [128, 4 * C], "int32"), "adr": ("sbuf", [128, 4 * C], "int32"),
    "lout": ("sbuf", [128, 48], "uint16"), "lin": ("sbuf", [128, 48], "uint16"),
    "tbl": ("sbuf", [128, 4 * K], "bfloat16"), "zb": ("sbuf", [128, 512], "bfloat16"),
    "yb": ("sbuf", [128, 1536], "float32"), "part": ("sbuf", [128, 2 * NC], "float32"),
    "acc": ("psum", [128, 4096], "float32"),
}
for _t in (1, 2, 3):
    SCRATCH["off%d" % _t] = ("sbuf", [128, 48], "uint16")
for _i in range(6):
    SCRATCH["wt%d" % _i] = ("sbuf", [128, 1536], "bfloat16")
    SCRATCH["wq%d" % _i] = ("sbuf", [128, 384], F8)
    SCRATCH["ws%d" % _i] = ("sbuf", [128, 384], "uint8")
for _k in range(4):
    SCRATCH["eb%d" % _k] = ("sbuf", [128, 4 * NC], "bfloat16")
    SCRATCH["eq%d" % _k] = ("sbuf", [128, NC], F8)
    SCRATCH["es%d" % _k] = ("sbuf", [128, NC], "uint8")
    if _k:
        SCRATCH["rq%d" % _k] = ("sbuf", [128, NC], F8)
        SCRATCH["rs%d" % _k] = ("sbuf", [128, NC], "uint8")

SEMAPHORES = (["lx", "ly", "fz", "tbs", "iot", "ct", "cd", "ad", "lo", "lown", "larr", "lsent", "esent",
               "pr", "rv", "pb", "vb", "sf", "vf", "ys"]
              + ["%s%d" % (n, k) for n in ("gv", "gs", "qe", "oo", "oi", "arr") for k in range(4)]
              + ["%s%d" % (n, i) for n in ("fw", "dw", "qw") for i in range(6)]
              + ["pp%d" % b for b in range(9)])

ADD, MUL, AND = AluOpType.add, AluOpType.mult, AluOpType.bitwise_and
COPY = ActivationFunctionType.Copy


def rank_program(g, core, T, topo):
    r = T.rank_of(core)
    if r is None:
        return
    S = T.sem
    V, A, P, Y = g.vector, g.scalar, g.tensor, g.sync
    ks = sorted((1, 2, 3), key=lambda k: topo.same_plane(topo.chip(core), topo.chip(T.cores[r ^ k])))
    k1, k2, k3 = ks
    q1, q2, q3 = [r ^ k for k in ks]
    tiles = [{r, q1}, {r, q2}, {r, q3}, {q1, q2}, {q1, q3}, {q2, q3}]
    dsts = [T.cores[q] for q in (q1, q2, q3)]
    engs = [e for e in topo.engines(core, dsts[0]) if all(e in topo.engines(core, d) for d in dsts)]
    ne = len(engs)
    mask = sum(1 << e for e in engs)
    parts = [engs[0::2], engs[1::4], engs[3::4]]

    for s in range(4):
        for l in range(2):
            p = 32 * s + 16 * l
            if s < 3:
                m = M0[s]
                Y.dma_start(T.cxy[p:p + 16, 0:C], T.px[:, m:m + C]).then_inc(S.lx, 16)
                A.dma_start(T.cxy[p:p + 16, C:2 * C], T.py[:, m:m + C]).then_inc(S.ly, 16)
            else:
                Y.dma_start(T.cxy[p:p + 16, 0:32], T.px[:]).then_inc(S.lx, 16)
                A.dma_start(T.cxy[p:p + 16, 32:64], T.py[:]).then_inc(S.ly, 16)
    for s in range(4):
        q = r if s != r else (r + 1) % N
        Y.dma_start(T.tbl[32 * s:32 * s + 32, :], T.tb[32 * q:32 * q + 32, :]).then_inc(S.tbs, 16)

    def wload(i, n):
        Y.wait_ge(S["fw%d" % i], n)
        a, b = sorted(tiles[i])
        for q, s in ((a, b), (b, a)):
            Y.dma_start(T["wt%d" % i][32 * s:32 * s + 32, :], T.w[32 * q:32 * q + 32, :]).then_inc(S["dw%d" % i], 16)

    wload(0, 1)
    wload(2, 3)
    wload(1, 2)
    Y.wait_ge(S.lsent, ne)
    for i, n in ((3, 3), (4, 3), (5, 1)):
        wload(i, n)

    g.iota(T.pw[:], [[0, 16]], 0, 1).then_inc(S.iot, 1)
    trs = []
    for k, q, d, es in zip(ks, (q1, q2, q3), dsts, parts):
        rid, pid, _ = topo.addr(d)
        trs.append(RemoteDMATransfer(
            dst_ids=[DstId(rid=rid, pnc=pid)], dma_engine_mask=sum(1 << e for e in es), remote_sem=S.larr,
            srcs=[T.lout[:, 12 * q:12 * q + 12]], dsts=[T.lin[:, 12 * k:12 * k + 12]]))
    g.wait_ge(S.lo, 3)
    g.remote_dma_fused(trs, local_sem=S.lsent)
    for k, d in zip(ks, dsts):
        rid, pid, _ = topo.addr(d)
        g.wait_ge(S["qe%d" % k], 1)
        g.remote_dma(T["rq%d" % k][:].bitcast(dt.uint8), T["eq%d" % k][:].bitcast(dt.uint8), S["arr%d" % k], S.esent, pid, rid, mask)
        g.remote_dma(T["rs%d" % k][:], T["es%d" % k][:], S["arr%d" % k], S.esent, pid, rid, mask)
    g.wait_ge(S.esent, 6 * ne)

    V.memset(T.zb[:], 0.0).then_inc(S.fz, 1)
    V.memset(T.wt0[:], 0.0).then_inc(S.fw0, 1)
    V.memset(T.lout[:], 0).then_inc(S.cd, 1)
    V.memset(T.xs[96:128, :], 0).then_inc(S.cd, 1)
    V.wait_ge(S.iot, 1)
    V.tensor_scalar(T.lw[:], T.pw[:], 16, None, AND).then_inc(S.ct, 1)
    V.wait_ge(S.ct, 1)
    for q in range(N):
        a, b = 2 * q, 2 * q + 1
        V.tensor_scalar(T.sc[:, q:q + 1], T.lw[:, 0:1], 2.0 ** -SH[a] / 16.0, 2.0 ** -SH[a], MUL, ADD).then_inc(S.cd, 1)
        for c, M in ((0, MA), (4 * C, MB)):
            V.tensor_scalar(T.ab[:, c + q:c + 4 * C:4], T.lw[:, 0:C], (M[b] - M[a]) / 4.0, 4.0 * M[a], MUL, ADD).then_inc(S.cd, 1)
    V.wait_ge(S.cd, 14)
    V.tensor_scalar(T.bc[:], T.sc[:], 0.5, -0.5, MUL, ADD).then_inc(S.cd, 1)
    V.memset(T.wt1[:, 0:512], 0.0).then_inc(S.fw1, 1)
    V.wait_ge(S.cd, 15)
    V.wait_ge(S.lx, 128)
    V.wait_ge(S.ly, 128)
    for q in range(N):
        V.tensor_scalar(T.xs[0:96, q:8 * C:4], T.cxy[0:96, 0:2 * C], T.sc[0:96, q:q + 1], T.bc[0:96, q:q + 1], MUL, ADD).then_inc(S.ad, 1)
        if q < 3:
            m = M0[q]
            for c, x in ((0, m), (4 * C, 32 + m)):
                V.tensor_scalar(T.xs[96:128, c + q:c + 4 * C:4], T.cxy[96:128, x:x + C], T.sc[96:128, q:q + 1], T.bc[96:128, q:q + 1], MUL, ADD).then_inc(S.ad, 1)
    V.wait_ge(S.ad, 10)
    V.tensor_tensor(T.xm[:], T.xs[:], T.ab[:], MUL).then_inc(S.ad, 1)
    V.wait_ge(S.ad, 11)
    V.tensor_tensor(T.xa[:], T.xm[:, 0:4 * C], T.xm[:, 4 * C:8 * C], ADD).then_inc(S.ad, 1)
    V.wait_ge(S.ad, 12)
    V.tensor_scalar(T.adr[:], T.xa[:], 4 * (K - 1), None, AND).then_inc(S.ad, 1)
    V.wait_ge(S.ad, 13)
    for q in (q1, q2, q3, r):
        V.tensor_copy(T.lout[:, 12 * q:12 * q + C], T.adr[:, q:4 * C:4]).then_inc(S.lown if q == r else S.lo, 1)
    V.memset(T.wt1[:, 512:1536], 0.0).then_inc(S.fw1, 1)

    def offs(t, k):
        c = 12 * k
        if t:
            return T["off%d" % t][:, c:c + C]
        return T.lin[:, c:c + C] if k else T.lout[:, 12 * r:12 * r + C]

    V.wait_ge(S.lown, 1)
    for t in (3, 1, 2):
        V.tensor_scalar(T["off%d" % t][:, 0:12], T.lout[:, 12 * r:12 * r + 12], float(t), None, ADD).then_inc(S["oo%d" % t], 1)

    def vg(k):
        for t in (1, 2):
            V.tensor_copy(T["eb%d" % k][:, t:4 * NC:4], T.tbl[:].indirect(offs(t, k))).then_inc(S["gv%d" % k], 1)

    def vq(k):
        if k:
            V.wait_ge(S["gv%d" % k], 2)
        V.wait_ge(S["gs%d" % k], 2 if k else 4)
        V.quantize_mx(T["eq%d" % k][:], T["es%d" % k][:], T["eb%d" % k][:]).then_inc(S["qe%d" % k], 1)

    def vw(i):
        V.wait_ge(S["dw%d" % i], 32)
        V.quantize_mx(T["wq%d" % i][:], T["ws%d" % i][:], T["wt%d" % i][:]).then_inc(S["qw%d" % i], 1)

    vw(0)
    vw(2)
    V.memset(T.wt5[:], 0.0).then_inc(S.fw5, 1)
    vq(0)
    vw(1)
    V.wait_ge(S.tbs, 64)
    V.wait_ge(S.larr, ne)
    for t in (3, 1, 2):
        V.tensor_scalar(T["off%d" % t][:, 12:48], T.lin[:, 12:48], float(t), None, ADD).then_inc(S["oi%d" % t], 1)
    V.wait_ge(S.oi1, 1)
    V.wait_ge(S.oi2, 1)
    for k in ks:
        vg(k)
        vq(k)
    for i in (3, 4, 5):
        vw(i)

    A.wait_ge(S.fz, 1)
    for i in (2, 3, 4):
        for c in range(0, 1536, 512):
            A.activation(T["wt%d" % i][:, c:c + 512], T.zb[:], COPY).then_inc(S["fw%d" % i], 1)
    A.wait_ge(S.tbs, 64)

    def ag(k, t):
        A.activation(T["eb%d" % k][:, t:4 * NC:4], T.tbl[:].indirect(offs(t, k)), COPY).then_inc(S["gs%d" % k], 1)

    A.wait_ge(S.lown, 1)
    ag(0, 0)
    for t in (3, 1, 2):
        A.wait_ge(S["oo%d" % t], 1)
        ag(0, t)
    A.wait_ge(S.larr, ne)
    for n, k in enumerate(ks):
        ag(k, 0)
        if n == 0:
            A.wait_ge(S.oi3, 1)
        ag(k, 3)

    seq = [(0, 2), (0, 0), (0, 1), (1, 0), (1, 2), (1, 1), (2, 0), (2, 1), (2, 2)]
    pas = [(0, 2), (1, 2)]
    keep = [x for x in seq if x not in pas]

    def base(x):
        return 512 * (7 if x in pas else keep.index(x))

    seen = []

    def mm(k, x, first, last):
        e, z = ("rq%d", "rs%d") if k else ("eq%d", "es%d")
        o, th = x
        q = r ^ k
        s = 3 if (th == q and q < 3) else th
        i = tiles.index({q, s})
        if i not in seen:
            seen.append(i)
            P.wait_ge(S["qw%d" % i], 1)
        c = slice(128 * o, 128 * o + 128)
        b = base(x)
        return P.matmul_mx(T.acc[:, b:b + NC], T["wq%d" % i][:, c], T["ws%d" % i][:, c], T[e % k][:], T[z % k][:], first, last)

    P.wait_ge(S.qe0, 1)
    for x in seq:
        if x in pas:
            if x == pas[1]:
                P.wait_ge(S.rv, 1)
            mm(0, x, True, True).then_inc(S.pr, 1)
        else:
            mm(0, x, True, False)
    P.wait_ge(S["arr%d" % k1], 2 * ne)
    for x in keep:
        mm(k1, x, False, False)
    P.wait_ge(S["arr%d" % k2], 2 * ne)
    for x in seq:
        if x in pas:
            if x == pas[0]:
                P.wait_ge(S.rv, 2)
            else:
                P.wait_ge(S.vb, 1)
            mm(k1, x, True, False)
            mm(k2, x, False, True).then_inc(S.pb, 1)
        else:
            mm(k2, x, False, False)
    P.wait_ge(S["arr%d" % k3], 2 * ne)
    for n, x in enumerate(seq):
        if x in pas:
            if x == pas[0]:
                P.wait_ge(S.vb, 2)
            else:
                P.wait_ge(S.vf, 1)
        mm(k3, x, x in pas, True).then_inc(S["pp%d" % n], 1)

    for i in range(2):
        A.wait_ge(S.pr, i + 1)
        A.activation(T.part[:, NC * i:NC * i + NC], T.acc[:, 3584:3584 + NC], COPY).then_inc(S.rv, 1)
    for i in range(2):
        pi = T.part[:, NC * i:NC * i + NC]
        V.wait_ge(S.pb, i + 1)
        V.wait_ge(S.rv, i + 1)
        V.tensor_tensor(pi, T.acc[:, 3584:3584 + NC], pi, ADD).then_inc(S.vb, 1)
    cnt = {"s": 0, "v": 0}
    done = {}
    for n, x in enumerate(seq):
        o, th = x
        lo = 0 if th < 2 else 16 * (M0[1] + C - M0[2])
        y = T.yb[:, 512 * o + 16 * M0[th] + lo:512 * o + 16 * M0[th] + NC]
        b = base(x)
        a = T.acc[:, b + lo:b + NC]
        if x in pas:
            i = pas.index(x)
            V.wait_ge(S["pp%d" % n], 1)
            V.wait_ge(S.vb, i + 1)
            V.tensor_tensor(y, a, T.part[:, NC * i + lo:NC * i + NC], ADD).then_inc(S.vf, 1)
            cnt["v"] += 1
        elif n % 2:
            A.wait_ge(S["pp%d" % n], 1)
            A.activation(y, a, COPY).then_inc(S.sf, 1)
            cnt["s"] += 1
        else:
            V.wait_ge(S["pp%d" % n], 1)
            V.tensor_copy(y, a).then_inc(S.vf, 1)
            cnt["v"] += 1
        done[o] = (cnt["s"], cnt["v"])
    for o in range(O):
        Y.wait_ge(S.sf, done[o][0])
        Y.wait_ge(S.vf, done[o][1])
        Y.dma_start(T.y[:, 512 * o:512 * o + 512], T.yb[:, 512 * o:512 * o + 512]).then_inc(S.ys, 16)
    Y.wait_ge(S.ys, 16 * O)
